import numpy as np
import ml_dtypes


def mxq(x, axis, fmt="e4m3"):
    dtype, down = {"e4m3": (ml_dtypes.float8_e4m3fn, 7), "e5m2": (ml_dtypes.float8_e5m2, 14)}[fmt]
    v = np.moveaxis(np.asarray(x, np.float32).astype(ml_dtypes.bfloat16).astype(np.float64), axis, -1)
    blocks = v.reshape(v.shape[:-1] + (-1, 32))
    amax = np.abs(blocks).max(-1, keepdims=True)
    byte = np.maximum(np.where(amax > 0, np.frexp(amax)[1] - 1 + 127, 0) - down, 1)
    scale = np.exp2(byte - 127.0)
    codes = (blocks / scale).astype(np.float32).astype(dtype).astype(np.float64)
    return np.moveaxis((codes * scale).reshape(v.shape), -1, axis)


WIDE = False


def mx_kscale(k):
    if not WIDE:
        return np.ones(k)
    levels = np.array([10, -10, 5, -5, 0])
    if k % 512:
        return np.exp2(np.random.permutation(np.resize(levels, k // 32))).repeat(32)
    a = np.empty((k // 512, 16))
    for p in range(k // 512):
        a[p, :8] = np.random.permutation(np.resize(levels, 8))
        for g in range(8):
            far = levels[np.abs(levels - a[p, g]) >= 10]
            a[p, g + 8] = far[np.random.randint(len(far))]
    return np.exp2(a.ravel()).repeat(32)


def f64(x):
    return np.asarray(x).astype(np.float64)


def striped8(idx):
    return np.asarray(idx).reshape(8, -1, 16).transpose(0, 2, 1).reshape(128, -1).astype(np.uint16)


def unstriped8(offs):
    return offs.reshape(8, 16, -1).transpose(0, 2, 1).reshape(8, -1).astype(np.int64)


def pick8(x, idx, run):
    r = np.arange(len(x))
    return x[r[:, None], idx[r % (8 * run) // run]]


E2M1 = np.array([0.0, 0.5, 1.0, 1.5, 2.0, 3.0, 4.0, 6.0, -0.0, -0.5, -1.0, -1.5, -2.0, -3.0, -4.0, -6.0])


def pack_weight(w, fmt):
    k, n = w.shape
    w = f64(np.asarray(w, np.float32).astype(ml_dtypes.bfloat16)).reshape(k // 32, 32, n)
    amax = np.abs(w).max(1)
    if fmt == "e4m3":
        byte = np.frexp(amax)[1] - 1 + 127 - 7
    else:
        mant, ex = np.frexp(amax / 6.0)
        byte = np.where(mant > 0.5, ex, ex - 1) + 127
    byte = np.clip(np.where(amax > 0, byte, 1), 1, 254)
    scaled = (w * np.exp2(127.0 - byte)[:, None, :]).reshape(k, n).astype(np.float32)
    by_word = np.ascontiguousarray(scaled.reshape(k // 512, 128, 4, n).transpose(0, 1, 3, 2))
    if fmt == "e4m3":
        words = by_word.astype(ml_dtypes.float8_e4m3fn).view(np.uint8)
    else:
        c = by_word.astype(ml_dtypes.float4_e2m1fn).view(np.uint8) & 0xF
        words = (c[..., 0::2] | (c[..., 1::2] << 4)).reshape(k // 512, 128, 2 * n)
    return np.ascontiguousarray(words), np.ascontiguousarray(byte.astype(np.uint8).reshape(k // 512, 16, n))


def unpack_weight(words, scales, fmt):
    g, _, n = scales.shape
    words = np.ascontiguousarray(words).reshape(g, 128, n, -1)
    if fmt == "e4m3":
        vals = words.view(ml_dtypes.float8_e4m3fn).astype(np.float64)
    else:
        nib = np.empty((g, 128, n, 4), np.uint8)
        nib[..., 0::2] = words & 0xF
        nib[..., 1::2] = words >> 4
        vals = E2M1[nib]
    vals = vals * np.repeat(np.exp2(scales.astype(np.float64) - 127.0), 8, axis=1)[..., None]
    return vals.transpose(0, 1, 3, 2).reshape(g * 512, n)


D, T, I, Q = 512, 1024, 512, 128


def setup_inputs():
    n = np.random.standard_normal
    idx = np.stack([np.random.permutation(T)[:I] for _ in range(8)])
    idx2 = np.stack([np.random.permutation(T)[:I] for _ in range(8)])
    idx3 = np.stack([np.random.permutation(T)[:I] for _ in range(8)])
    fd = mx_kscale(D)
    keysp = pack_weight(n((D, T)) / fd[:, None], "e2m1")
    return {
        "query": (n((D, Q)) * 0.9 / np.sqrt(D) * fd[:, None]).astype(np.float32),
        "query2": (n((D, Q)) * 0.9 / np.sqrt(D) * fd[:, None]).astype(np.float32),
        "keys_words": keysp[0],
        "keys_scales": keysp[1],
        "lam": (np.random.uniform(0.5, 1.5, (Q, 1))).astype(np.float32),
        "old": (1.0 * n((Q, T))).astype(np.float32),
        "offs": striped8(idx),
        "offs2": striped8(idx2),
        "offs3": striped8(idx3),
    }


def reference(query, query2, keys_words, keys_scales, lam, old, offs, offs2, offs3):
    idx = unstriped8(offs)
    idx2 = unstriped8(offs2)
    idx3 = unstriped8(offs3)
    keysu = unpack_weight(keys_words, keys_scales, "e2m1")
    queryq = mxq(f64(query), 0, "e4m3")
    a = queryq.T @ keysu
    query2q = mxq(f64(query2), 0, "e4m3")
    b = query2q.T @ keysu
    w = pick8(a, idx, 16) + pick8(a, idx2, 16) * np.tanh(pick8(b, idx, 16)) * f64(lam)
    f1 = np.zeros((Q, T))
    f1[np.arange(Q)[:, None], idx[np.arange(Q) % 128 // 16]] = w
    f2 = f1 + f64(old)
    y = pick8(f2, idx3, 16) * w
    return y

@@ -1,0 +1,132 @@
+import concourse.mybir as mybir
+
+D, T, I, Q = 512, 1024, 512, 128
+FLOPS = 2 * 2 * D * Q * T
+
+F32 = mybir.dt.float32
+BF16 = mybir.dt.bfloat16
+I32 = mybir.dt.int32
+U32 = mybir.dt.uint32
+U16 = mybir.dt.uint16
+U8 = mybir.dt.uint8
+FP8X4 = mybir.dt.float8_e4m3fn_x4
+FP4X4 = mybir.dt.float4_e2m1fn_x4
+MULT = mybir.AluOpType.mult
+ADD = mybir.AluOpType.add
+COPY = mybir.ActivationFunctionType.Copy
+TANH = mybir.ActivationFunctionType.Tanh
+
+P = 128
+PACK = 4
+N = 256
+HALF = I // 2
+PER_COL = 16
+
+
+def tile_attend_turnedby_lean_throughtimes_heads_kernel(
+    tc, query, query2, keys_words, keys_scales, lam, old, offs, offs2, offs3, out
+):
+    nc = tc.nc
+    with (
+        tc.tile_pool(name="keep", bufs=1) as keep,
+        tc.psum_pool(name="psum", bufs=1) as psum,
+    ):
+        list1 = keep.tile([P, I // PER_COL], U16, name="list1")
+        list2 = keep.tile([P, I // PER_COL], U16, name="list2")
+        list3 = keep.tile([P, I // PER_COL], U16, name="list3")
+        raw_b = keep.tile([P, PACK, Q], F32, name="raw_b")
+        raw_a = keep.tile([P, PACK, Q], F32, name="raw_a")
+        key_words = keep.tile([P, 2 * T], U8, name="key_words", align_bytes=64)
+        key_scales = keep.tile([P, T], U8, name="key_scales", align_bytes=64)
+        lam_sb = keep.tile([P, 1], F32, name="lam_sb")
+        old_sb = keep.tile([P, T], F32, name="old_sb")
+        f1 = keep.tile([P, T], F32, name="f1")
+        f2 = keep.tile([P, T], F32, name="f2")
+        a_sb = keep.tile([P, T], F32, name="a_sb")
+        b_sb = keep.tile([P, T], F32, name="b_sb")
+
+        nc.vector.memset(key_scales[:].bitcast(I32), 0)
+        nc.sync.dma_start(raw_b[:], query2.rearrange("(p j) q -> p j q", j=PACK))
+        for quad in range(4):
+            nc.scalar.dma_start(
+                key_scales[32 * quad : 32 * quad + 4, :].bitcast(I32),
+                keys_scales[0, 4 * quad : 4 * quad + 4, :].bitcast(I32),
+            )
+        nc.sync.dma_start(key_words[:].bitcast(I32), keys_words[0].bitcast(I32))
+        nc.sync.dma_start(raw_a[:], query.rearrange("(p j) q -> p j q", j=PACK))
+        nc.sync.dma_start(list1[:], offs)
+        nc.sync.dma_start(list2[:], offs2)
+        nc.sync.dma_start(lam_sb[:], lam)
+        nc.sync.dma_start(old_sb[:], old)
+        nc.sync.dma_start(list3[:], offs3)
+        nc.vector.memset(f1[:], 0.0)
+
+        def quantize(raw, name):
+            grouped = keep.tile([P, Q, PACK], BF16, name=name + "_grouped", align_bytes=64)
+            codes = keep.tile([P, Q], U32, name=name + "_codes", align_bytes=64)
+            scales = keep.tile([P, Q], U8, name=name + "_scales", align_bytes=64)
+            nc.vector.tensor_copy(grouped[:], raw[:].rearrange("p j q -> p q j"))
+            nc.vector.quantize_mx(
+                out=codes[:].bitcast(FP8X4),
+                scales=scales[:],
+                in_=grouped[:].rearrange("p q j -> p (q j)"),
+            )
+            return codes, scales
+
+        def scores(codes, scales, name):
+            banks = []
+            for c in range(T // N):
+                bank = psum.tile([P, N], F32, name=name + "_bank" + str(c))
+                nc.tensor.matmul_mx(
+                    out=bank[:],
+                    lhsT=codes[:].bitcast(FP8X4),
+                    lhsT_scale=scales[:],
+                    rhs=key_words[:, 2 * N * c : 2 * N * (c + 1)].bitcast(FP4X4),
+                    rhs_scale=key_scales[:, N * c : N * (c + 1)],
+                    start=True,
+                    stop=True,
+                )
+                banks.append(bank)
+            return banks
+
+        def half(lst, h):
+            cols = HALF // PER_COL
+            return lst[:, h * cols : (h + 1) * cols]
+
+        b_banks = scores(*quantize(raw_b, "qb"), "b")
+        a_banks = scores(*quantize(raw_a, "qa"), "a")
+        for c in range(T // N):
+            nc.scalar.activation(b_sb[:, N * c : N * (c + 1)], b_banks[c][:], COPY)
+        for c in range(T // N):
+            nc.vector.tensor_copy(a_sb[:, N * c : N * (c + 1)], a_banks[c][:])
+
+        def slots(name):
+            return [keep.tile([P, HALF], F32, name=name + str(h)) for h in range(2)]
+
+        b1, tanh_b, a1, lean, w, picked, y = (
+            slots(n) for n in ("b1_", "tanh_b", "a1_", "lean", "w", "picked", "y")
+        )
+        a2_second = keep.tile([P, HALF], F32, name="a2_second")
+
+        nc.scalar.activation(b1[0][:], b_sb[:].indirect(half(list1, 0)), COPY)
+        nc.scalar.activation(tanh_b[0][:], b1[0][:], TANH)
+        nc.scalar.activation(a1[0][:], a_sb[:].indirect(half(list1, 0)), COPY)
+        nc.vector.tensor_tensor(lean[0][:], a_sb[:].indirect(half(list2, 0)), tanh_b[0][:], MULT)
+        nc.vector.scalar_tensor_tensor(w[0][:], lean[0][:], lam_sb[:], a1[0][:], MULT, ADD)
+        nc.vector.tensor_copy(f1[:].indirect(half(list1, 0)), w[0][:])
+
+        nc.scalar.activation(b1[1][:], b_sb[:].indirect(half(list1, 1)), COPY)
+        nc.scalar.activation(a2_second[:], a_sb[:].indirect(half(list2, 1)), COPY)
+        nc.scalar.activation(tanh_b[1][:], b1[1][:], TANH)
+        nc.scalar.activation(a1[1][:], a_sb[:].indirect(half(list1, 1)), COPY)
+        nc.vector.tensor_tensor(lean[1][:], a2_second[:], tanh_b[1][:], MULT)
+        nc.vector.scalar_tensor_tensor(w[1][:], lean[1][:], lam_sb[:], a1[1][:], MULT, ADD)
+        nc.vector.tensor_copy(f1[:].indirect(half(list1, 1)), w[1][:])
+
+        nc.vector.tensor_tensor(f2[:], f1[:], old_sb[:], ADD)
+
+        nc.vector.tensor_tensor(y[0][:], f2[:].indirect(half(list3, 0)), w[0][:], MULT)
+        nc.sync.dma_start(out[:, 0:HALF], y[0][:])
+        nc.scalar.activation(picked[1][:], f2[:].indirect(half(list3, 1)), COPY)
+        nc.vector.tensor_tensor(y[1][:], picked[1][:], w[1][:], MULT)
+        nc.scalar.dma_start(out[:, HALF:I], y[1][:])

@@ -18,7 +18,10 @@ TANH = mybir.ActivationFunctionType.Tanh
 
 P = 128
 PACK = 4
-N = 256
+B_PIECES = (256, 256, 256, 256)
+A_PIECES = (256, 256, 256, 128, 128)
+BANKS = 8
+EARLY = 768
 HALF = I // 2
 PER_COL = 16
 
@@ -36,7 +39,7 @@ def tile_attend_turnedby_lean_throughtimes_heads_kernel(
         list3 = keep.tile([P, I // PER_COL], U16, name="list3")
         raw_b = keep.tile([P, PACK, Q], F32, name="raw_b")
         raw_a = keep.tile([P, PACK, Q], F32, name="raw_a")
-        key_words = keep.tile([P, 2 * T], U8, name="key_words", align_bytes=64)
+        key_words = [keep.tile([P, 2 * n], U8, name="key_words" + str(n), align_bytes=64) for n in (EARLY, T - EARLY)]
         key_scales = keep.tile([P, T], U8, name="key_scales", align_bytes=64)
         lam_sb = keep.tile([P, 1], F32, name="lam_sb")
         old_sb = keep.tile([P, T], F32, name="old_sb")
@@ -47,13 +50,16 @@ def tile_attend_turnedby_lean_throughtimes_heads_kernel(
 
         nc.vector.memset(key_scales[:].bitcast(I32), 0)
         nc.sync.dma_start(raw_b[:], query2.rearrange("(p j) q -> p j q", j=PACK))
-        for quad in range(4):
-            nc.scalar.dma_start(
-                key_scales[32 * quad : 32 * quad + 4, :].bitcast(I32),
-                keys_scales[0, 4 * quad : 4 * quad + 4, :].bitcast(I32),
+        half_bytes = 2 * EARLY
+        words_in = keys_words[0]
+        nc.sync.dma_start(key_words[0][:].bitcast(I32), words_in[:, 0:half_bytes].bitcast(I32))
+        for r in range(4):
+            nc.sync.dma_start(
+                key_scales[r:P:32, :].bitcast(I32),
+                keys_scales[0, r:16:4, :].bitcast(I32),
             )
-        nc.sync.dma_start(key_words[:].bitcast(I32), keys_words[0].bitcast(I32))
         nc.sync.dma_start(raw_a[:], query.rearrange("(p j) q -> p j q", j=PACK))
+        nc.sync.dma_start(key_words[1][:].bitcast(I32), words_in[:, half_bytes : 2 * T].bitcast(I32))
         nc.sync.dma_start(list1[:], offs)
         nc.sync.dma_start(list2[:], offs2)
         nc.sync.dma_start(lam_sb[:], lam)
@@ -61,72 +67,89 @@ def tile_attend_turnedby_lean_throughtimes_heads_kernel(
         nc.sync.dma_start(list3[:], offs3)
         nc.vector.memset(f1[:], 0.0)
 
-        def quantize(raw, name):
-            grouped = keep.tile([P, Q, PACK], BF16, name=name + "_grouped", align_bytes=64)
+        def quantize(raw, name, parts):
             codes = keep.tile([P, Q], U32, name=name + "_codes", align_bytes=64)
             scales = keep.tile([P, Q], U8, name=name + "_scales", align_bytes=64)
-            nc.vector.tensor_copy(grouped[:], raw[:].rearrange("p j q -> p q j"))
-            nc.vector.quantize_mx(
-                out=codes[:].bitcast(FP8X4),
-                scales=scales[:],
-                in_=grouped[:].rearrange("p q j -> p (q j)"),
-            )
+            width = Q // parts
+            staged = []
+            for c in range(parts):
+                cols = slice(c * width, (c + 1) * width)
+                grouped = keep.tile([P, width, PACK], BF16, name=name + "_grouped" + str(c), align_bytes=64)
+                nc.vector.tensor_copy(grouped[:], raw[:, :, cols].rearrange("p j q -> p q j"))
+                staged.append((grouped, cols))
+            for grouped, cols in staged:
+                nc.vector.quantize_mx(
+                    out=codes[:, cols].bitcast(FP8X4),
+                    scales=scales[:, cols],
+                    in_=grouped[:].rearrange("p q j -> p (q j)"),
+                )
             return codes, scales
 
-        def scores(codes, scales, name):
+        def scores(codes, scales, name, pieces, first_bank):
             banks = []
-            for c in range(T // N):
-                bank = psum.tile([P, N], F32, name=name + "_bank" + str(c))
+            start = 0
+            for c, width in enumerate(pieces):
+                tag = "bank" + str((first_bank + c) % BANKS)
+                bank = psum.tile([P, width], F32, name=name + str(c), tag=tag)
                 nc.tensor.matmul_mx(
                     out=bank[:],
                     lhsT=codes[:].bitcast(FP8X4),
                     lhsT_scale=scales[:],
-                    rhs=key_words[:, 2 * N * c : 2 * N * (c + 1)].bitcast(FP4X4),
-                    rhs_scale=key_scales[:, N * c : N * (c + 1)],
+                    rhs=key_words[start // EARLY][:, 2 * (start % EARLY) : 2 * (start % EARLY + width)].bitcast(FP4X4),
+                    rhs_scale=key_scales[:, start : start + width],
                     start=True,
                     stop=True,
                 )
-                banks.append(bank)
+                banks.append((bank, slice(start, start + width)))
+                start = start + width
             return banks
 
         def half(lst, h):
             cols = HALF // PER_COL
             return lst[:, h * cols : (h + 1) * cols]
 
-        b_banks = scores(*quantize(raw_b, "qb"), "b")
-        a_banks = scores(*quantize(raw_a, "qa"), "a")
-        for c in range(T // N):
-            nc.scalar.activation(b_sb[:, N * c : N * (c + 1)], b_banks[c][:], COPY)
-        for c in range(T // N):
-            nc.vector.tensor_copy(a_sb[:, N * c : N * (c + 1)], a_banks[c][:])
+        for bank, cols in scores(*quantize(raw_b, "qb", 2), "b", B_PIECES, 0):
+            nc.scalar.activation(b_sb[:, cols], bank[:], COPY)
+        a_banks = scores(*quantize(raw_a, "qa", 2), "a", A_PIECES, len(B_PIECES))
+        for bank, cols in a_banks[:2]:
+            nc.vector.tensor_copy(a_sb[:, cols], bank[:])
+        for bank, cols in a_banks[2:]:
+            nc.scalar.activation(a_sb[:, cols], bank[:], COPY)
 
-        def slots(name):
-            return [keep.tile([P, HALF], F32, name=name + str(h)) for h in range(2)]
+        def slot_tile(name, tag=None):
+            return keep.tile([P, HALF], F32, name=name, tag=tag or name)
 
-        b1, tanh_b, a1, lean, w, picked, y = (
-            slots(n) for n in ("b1_", "tanh_b", "a1_", "lean", "w", "picked", "y")
-        )
-        a2_second = keep.tile([P, HALF], F32, name="a2_second")
+        b1_0, b1_1 = slot_tile("b1_0"), slot_tile("b1_1")
+        tanh_0, tanh_1 = slot_tile("tanh_0"), slot_tile("tanh_1", "tanh_1_then_w_0")
+        a1_0, a1_1 = slot_tile("a1_0"), slot_tile("a1_1")
+        a2_0 = slot_tile("a2_0", "a2")
+        lean_0, lean_1 = slot_tile("lean_0"), slot_tile("lean_1")
 
-        nc.scalar.activation(b1[0][:], b_sb[:].indirect(half(list1, 0)), COPY)
-        nc.scalar.activation(tanh_b[0][:], b1[0][:], TANH)
-        nc.scalar.activation(a1[0][:], a_sb[:].indirect(half(list1, 0)), COPY)
-        nc.vector.tensor_tensor(lean[0][:], a_sb[:].indirect(half(list2, 0)), tanh_b[0][:], MULT)
-        nc.vector.scalar_tensor_tensor(w[0][:], lean[0][:], lam_sb[:], a1[0][:], MULT, ADD)
-        nc.vector.tensor_copy(f1[:].indirect(half(list1, 0)), w[0][:])
+        nc.vector.tensor_copy(b1_0[:], b_sb[:].indirect(half(list1, 0)))
+        nc.scalar.activation(tanh_0[:], b1_0[:], TANH)
+        nc.scalar.activation(a1_0[:], a_sb[:].indirect(half(list1, 0)), COPY)
+        nc.vector.tensor_copy(a2_0[:], a_sb[:].indirect(half(list2, 0)))
+        nc.vector.scalar_tensor_tensor(lean_0[:], a2_0[:], lam_sb[:], tanh_0[:], MULT, MULT)
+        nc.vector.tensor_tensor(f1[:].indirect(half(list1, 0)), lean_0[:], a1_0[:], ADD)
 
-        nc.scalar.activation(b1[1][:], b_sb[:].indirect(half(list1, 1)), COPY)
-        nc.scalar.activation(a2_second[:], a_sb[:].indirect(half(list2, 1)), COPY)
-        nc.scalar.activation(tanh_b[1][:], b1[1][:], TANH)
-        nc.scalar.activation(a1[1][:], a_sb[:].indirect(half(list1, 1)), COPY)
-        nc.vector.tensor_tensor(lean[1][:], a2_second[:], tanh_b[1][:], MULT)
-        nc.vector.scalar_tensor_tensor(w[1][:], lean[1][:], lam_sb[:], a1[1][:], MULT, ADD)
-        nc.vector.tensor_copy(f1[:].indirect(half(list1, 1)), w[1][:])
+        a2_1 = slot_tile("a2_1", "a2")
+        nc.scalar.activation(b1_1[:], b_sb[:].indirect(half(list1, 1)), COPY)
+        nc.scalar.activation(a2_1[:], a_sb[:].indirect(half(list2, 1)), COPY)
+        nc.scalar.activation(tanh_1[:], b1_1[:], TANH)
+        nc.scalar.activation(a1_1[:], a_sb[:].indirect(half(list1, 1)), COPY)
+        nc.vector.scalar_tensor_tensor(lean_1[:], a2_1[:], lam_sb[:], tanh_1[:], MULT, MULT)
+        w_0 = slot_tile("w_0", "tanh_1_then_w_0")
+        w_1 = slot_tile("w_1")
+        nc.vector.tensor_tensor(w_0[:], lean_0[:], a1_0[:], ADD)
+        nc.vector.tensor_tensor(f1[:].indirect(half(list1, 1)), lean_1[:], a1_1[:], ADD)
+        nc.vector.tensor_tensor(w_1[:], lean_1[:], a1_1[:], ADD)
 
         nc.vector.tensor_tensor(f2[:], f1[:], old_sb[:], ADD)
 
-        nc.vector.tensor_tensor(y[0][:], f2[:].indirect(half(list3, 0)), w[0][:], MULT)
-        nc.sync.dma_start(out[:, 0:HALF], y[0][:])
-        nc.scalar.activation(picked[1][:], f2[:].indirect(half(list3, 1)), COPY)
-        nc.vector.tensor_tensor(y[1][:], picked[1][:], w[1][:], MULT)
-        nc.scalar.dma_start(out[:, HALF:I], y[1][:])
+        picked = slot_tile("picked")
+        y_0, y_1 = slot_tile("y_0"), slot_tile("y_1")
+        nc.vector.tensor_tensor(y_0[:], f2[:].indirect(half(list3, 0)), w_0[:], MULT)
+        nc.scalar.dma_start(out[:, 0:HALF], y_0[:])
+        nc.scalar.activation(picked[:], f2[:].indirect(half(list3, 1)), COPY)
+        nc.vector.tensor_tensor(y_1[:], picked[:], w_1[:], MULT)
+        nc.sync.dma_start(out[:, HALF:I], y_1[:])

@@ -21,7 +21,7 @@ PACK = 4
 B_PIECES = (256, 256, 256, 256)
 A_PIECES = (256, 256, 256, 128, 128)
 BANKS = 8
-EARLY = 768
+EARLY = 512
 HALF = I // 2
 PER_COL = 16
 
@@ -39,7 +39,7 @@ def tile_attend_turnedby_lean_throughtimes_heads_kernel(
         list3 = keep.tile([P, I // PER_COL], U16, name="list3")
         raw_b = keep.tile([P, PACK, Q], F32, name="raw_b")
         raw_a = keep.tile([P, PACK, Q], F32, name="raw_a")
-        key_words = [keep.tile([P, 2 * n], U8, name="key_words" + str(n), align_bytes=64) for n in (EARLY, T - EARLY)]
+        key_words = [keep.tile([P, 2 * n], U8, name="key_words" + str(h), align_bytes=64) for h, n in enumerate((EARLY, T - EARLY))]
         key_scales = keep.tile([P, T], U8, name="key_scales", align_bytes=64)
         lam_sb = keep.tile([P, 1], F32, name="lam_sb")
         old_sb = keep.tile([P, T], F32, name="old_sb")
@@ -54,7 +54,8 @@ def tile_attend_turnedby_lean_throughtimes_heads_kernel(
         words_in = keys_words[0]
         nc.sync.dma_start(key_words[0][:].bitcast(I32), words_in[:, 0:half_bytes].bitcast(I32))
         for r in range(4):
-            nc.sync.dma_start(
+            queue = nc.sync if r < 3 else nc.scalar
+            queue.dma_start(
                 key_scales[r:P:32, :].bitcast(I32),
                 keys_scales[0, r:16:4, :].bitcast(I32),
             )

import concourse.mybir as mybir

D, T, I, Q = 512, 1024, 512, 128
FLOPS = 2 * 2 * D * Q * T

F32 = mybir.dt.float32
BF16 = mybir.dt.bfloat16
I32 = mybir.dt.int32
U32 = mybir.dt.uint32
U16 = mybir.dt.uint16
U8 = mybir.dt.uint8
FP8X4 = mybir.dt.float8_e4m3fn_x4
FP4X4 = mybir.dt.float4_e2m1fn_x4
MULT = mybir.AluOpType.mult
ADD = mybir.AluOpType.add
COPY = mybir.ActivationFunctionType.Copy
TANH = mybir.ActivationFunctionType.Tanh

P = 128
PACK = 4
B_PIECES = (256, 256, 256, 256)
A_PIECES = (256, 256, 256, 128, 128)
BANKS = 8
EARLY = 512
HALF = I // 2
PER_COL = 16


def tile_attend_turnedby_lean_throughtimes_heads_kernel(
    tc, query, query2, keys_words, keys_scales, lam, old, offs, offs2, offs3, out
):
    nc = tc.nc
    with (
        tc.tile_pool(name="keep", bufs=1) as keep,
        tc.psum_pool(name="psum", bufs=1) as psum,
    ):
        list1 = keep.tile([P, I // PER_COL], U16, name="list1")
        list2 = keep.tile([P, I // PER_COL], U16, name="list2")
        list3 = keep.tile([P, I // PER_COL], U16, name="list3")
        raw_b = keep.tile([P, PACK, Q], F32, name="raw_b")
        raw_a = keep.tile([P, PACK, Q], F32, name="raw_a")
        key_words = [keep.tile([P, 2 * n], U8, name="key_words" + str(h), align_bytes=64) for h, n in enumerate((EARLY, T - EARLY))]
        key_scales = keep.tile([P, T], U8, name="key_scales", align_bytes=64)
        lam_sb = keep.tile([P, 1], F32, name="lam_sb")
        old_sb = keep.tile([P, T], F32, name="old_sb")
        f1 = keep.tile([P, T], F32, name="f1")
        f2 = keep.tile([P, T], F32, name="f2")
        a_sb = keep.tile([P, T], F32, name="a_sb")
        b_sb = keep.tile([P, T], F32, name="b_sb")

        nc.vector.memset(key_scales[:].bitcast(I32), 0)
        nc.sync.dma_start(raw_b[:], query2.rearrange("(p j) q -> p j q", j=PACK))
        half_bytes = 2 * EARLY
        words_in = keys_words[0]
        nc.sync.dma_start(key_words[0][:].bitcast(I32), words_in[:, 0:half_bytes].bitcast(I32))
        for r in range(4):
            queue = nc.sync if r < 3 else nc.scalar
            queue.dma_start(
                key_scales[r:P:32, :].bitcast(I32),
                keys_scales[0, r:16:4, :].bitcast(I32),
            )
        nc.sync.dma_start(raw_a[:], query.rearrange("(p j) q -> p j q", j=PACK))
        nc.sync.dma_start(key_words[1][:].bitcast(I32), words_in[:, half_bytes : 2 * T].bitcast(I32))
        nc.sync.dma_start(list1[:], offs)
        nc.sync.dma_start(list2[:], offs2)
        nc.sync.dma_start(lam_sb[:], lam)
        nc.sync.dma_start(old_sb[:], old)
        nc.sync.dma_start(list3[:], offs3)
        nc.vector.memset(f1[:], 0.0)

        def quantize(raw, name, parts):
            codes = keep.tile([P, Q], U32, name=name + "_codes", align_bytes=64)
            scales = keep.tile([P, Q], U8, name=name + "_scales", align_bytes=64)
            width = Q // parts
            staged = []
            for c in range(parts):
                cols = slice(c * width, (c + 1) * width)
                grouped = keep.tile([P, width, PACK], BF16, name=name + "_grouped" + str(c), align_bytes=64)
                nc.vector.tensor_copy(grouped[:], raw[:, :, cols].rearrange("p j q -> p q j"))
                staged.append((grouped, cols))
            for grouped, cols in staged:
                nc.vector.quantize_mx(
                    out=codes[:, cols].bitcast(FP8X4),
                    scales=scales[:, cols],
                    in_=grouped[:].rearrange("p q j -> p (q j)"),
                )
            return codes, scales

        def scores(codes, scales, name, pieces, first_bank):
            banks = []
            start = 0
            for c, width in enumerate(pieces):
                tag = "bank" + str((first_bank + c) % BANKS)
                bank = psum.tile([P, width], F32, name=name + str(c), tag=tag)
                nc.tensor.matmul_mx(
                    out=bank[:],
                    lhsT=codes[:].bitcast(FP8X4),
                    lhsT_scale=scales[:],
                    rhs=key_words[start // EARLY][:, 2 * (start % EARLY) : 2 * (start % EARLY + width)].bitcast(FP4X4),
                    rhs_scale=key_scales[:, start : start + width],
                    start=True,
                    stop=True,
                )
                banks.append((bank, slice(start, start + width)))
                start = start + width
            return banks

        def half(lst, h):
            cols = HALF // PER_COL
            return lst[:, h * cols : (h + 1) * cols]

        for bank, cols in scores(*quantize(raw_b, "qb", 2), "b", B_PIECES, 0):
            nc.scalar.activation(b_sb[:, cols], bank[:], COPY)
        a_banks = scores(*quantize(raw_a, "qa", 2), "a", A_PIECES, len(B_PIECES))
        for bank, cols in a_banks[:2]:
            nc.vector.tensor_copy(a_sb[:, cols], bank[:])
        for bank, cols in a_banks[2:]:
            nc.scalar.activation(a_sb[:, cols], bank[:], COPY)

        def slot_tile(name, tag=None):
            return keep.tile([P, HALF], F32, name=name, tag=tag or name)

        b1_0, b1_1 = slot_tile("b1_0"), slot_tile("b1_1")
        tanh_0, tanh_1 = slot_tile("tanh_0"), slot_tile("tanh_1", "tanh_1_then_w_0")
        a1_0, a1_1 = slot_tile("a1_0"), slot_tile("a1_1")
        a2_0 = slot_tile("a2_0", "a2")
        lean_0, lean_1 = slot_tile("lean_0"), slot_tile("lean_1")

        nc.vector.tensor_copy(b1_0[:], b_sb[:].indirect(half(list1, 0)))
        nc.scalar.activation(tanh_0[:], b1_0[:], TANH)
        nc.scalar.activation(a1_0[:], a_sb[:].indirect(half(list1, 0)), COPY)
        nc.vector.tensor_copy(a2_0[:], a_sb[:].indirect(half(list2, 0)))
        nc.vector.scalar_tensor_tensor(lean_0[:], a2_0[:], lam_sb[:], tanh_0[:], MULT, MULT)
        nc.vector.tensor_tensor(f1[:].indirect(half(list1, 0)), lean_0[:], a1_0[:], ADD)

        a2_1 = slot_tile("a2_1", "a2")
        nc.scalar.activation(b1_1[:], b_sb[:].indirect(half(list1, 1)), COPY)
        nc.scalar.activation(a2_1[:], a_sb[:].indirect(half(list2, 1)), COPY)
        nc.scalar.activation(tanh_1[:], b1_1[:], TANH)
        nc.scalar.activation(a1_1[:], a_sb[:].indirect(half(list1, 1)), COPY)
        nc.vector.scalar_tensor_tensor(lean_1[:], a2_1[:], lam_sb[:], tanh_1[:], MULT, MULT)
        w_0 = slot_tile("w_0", "tanh_1_then_w_0")
        w_1 = slot_tile("w_1")
        nc.vector.tensor_tensor(w_0[:], lean_0[:], a1_0[:], ADD)
        nc.vector.tensor_tensor(f1[:].indirect(half(list1, 1)), lean_1[:], a1_1[:], ADD)
        nc.vector.tensor_tensor(w_1[:], lean_1[:], a1_1[:], ADD)

        nc.vector.tensor_tensor(f2[:], f1[:], old_sb[:], ADD)

        picked = slot_tile("picked")
        y_0, y_1 = slot_tile("y_0"), slot_tile("y_1")
        nc.vector.tensor_tensor(y_0[:], f2[:].indirect(half(list3, 0)), w_0[:], MULT)
        nc.scalar.dma_start(out[:, 0:HALF], y_0[:])
        nc.scalar.activation(picked[:], f2[:].indirect(half(list3, 1)), COPY)
        nc.vector.tensor_tensor(y_1[:], picked[:], w_1[:], MULT)
        nc.sync.dma_start(out[:, HALF:I], y_1[:])
